import numpy as np
import ml_dtypes


def mxq(x, axis, fmt="e4m3"):
    dtype, down = {"e4m3": (ml_dtypes.float8_e4m3fn, 7), "e5m2": (ml_dtypes.float8_e5m2, 14)}[fmt]
    v = np.moveaxis(np.asarray(x, np.float32).astype(ml_dtypes.bfloat16).astype(np.float64), axis, -1)
    blocks = v.reshape(v.shape[:-1] + (-1, 32))
    amax = np.abs(blocks).max(-1, keepdims=True)
    byte = np.maximum(np.where(amax > 0, np.frexp(amax)[1] - 1 + 127, 0) - down, 1)
    scale = np.exp2(byte - 127.0)
    codes = (blocks / scale).astype(np.float32).astype(dtype).astype(np.float64)
    return np.moveaxis((codes * scale).reshape(v.shape), -1, axis)


WIDE = False


def mx_kscale(k):
    if not WIDE:
        return np.ones(k)
    levels = np.array([10, -10, 5, -5, 0])
    if k % 512:
        return np.exp2(np.random.permutation(np.resize(levels, k // 32))).repeat(32)
    a = np.empty((k // 512, 16))
    for p in range(k // 512):
        a[p, :8] = np.random.permutation(np.resize(levels, 8))
        for g in range(8):
            far = levels[np.abs(levels - a[p, g]) >= 10]
            a[p, g + 8] = far[np.random.randint(len(far))]
    return np.exp2(a.ravel()).repeat(32)


def f64(x):
    return np.asarray(x).astype(np.float64)


def striped(idx):
    return np.tile(idx.reshape(-1, 16).T, (8, 1)).astype(np.uint16)


def unstriped(offs):
    return offs[:16].T.reshape(-1).astype(np.int64)


def pack_weight(w):
    k, n = w.shape
    w = f64(np.asarray(w, np.float32).astype(ml_dtypes.bfloat16)).reshape(k // 32, 32, n)
    amax = np.abs(w).max(1)
    byte = np.clip(np.where(amax > 0, np.frexp(amax)[1] - 1 + 127 - 7, 1), 1, 254)
    scaled = (w * np.exp2(127.0 - byte)[:, None, :]).reshape(k, n).astype(np.float32)
    words = np.ascontiguousarray(scaled.reshape(k // 512, 128, 4, n).transpose(0, 1, 3, 2)).astype(ml_dtypes.float8_e4m3fn).view(np.uint8)
    return words, np.ascontiguousarray(byte.astype(np.uint8).reshape(k // 512, 16, n))


def unpack_weight(words, scales):
    g, p, n, _ = words.shape
    vals = np.ascontiguousarray(words).view(ml_dtypes.float8_e4m3fn).astype(np.float64) * np.repeat(np.exp2(scales.astype(np.float64) - 127.0), 8, axis=1)[..., None]
    return vals.transpose(0, 1, 3, 2).reshape(g * 512, n)


K, T, S, N, U = 512, 1024, 512, 128, 512
P = 2 ** 7


def setup_inputs():
    n = np.random.standard_normal
    s = mx_kscale(K)[:, None]
    packed_xT = pack_weight(n((K, T)) * s)
    return {
        "x_words": packed_xT[0],
        "x_scales": packed_xT[1],
        "w1": (n((K, N)) / np.sqrt(K) / s).astype(np.float32),
        "half": (np.tile(np.random.uniform(0.7, 1.3, U), (P, 1))).astype(np.float32),
        "tx": (n((N, U)) / np.sqrt(2)).astype(np.float32),
        "ty": (n((N, U)) / np.sqrt(2)).astype(np.float32),
        "offs": striped(np.random.permutation(T)[:S]),
        "xp": striped(np.random.permutation(S)),
        "xm": striped(np.random.permutation(S)),
        "yp": striped(np.random.permutation(S)),
        "ym": striped(np.random.permutation(S)),
    }


def reference(x_words, x_scales, w1, half, tx, ty, offs, xp, xm, yp, ym):
    xq = unpack_weight(x_words, x_scales)[:, unstriped(offs)]
    y = mxq(f64(w1), 0, "e4m3").T @ xq
    gx = f64(half)[:1] * (y[:, unstriped(xp)] - y[:, unstriped(xm)])
    gy = f64(half)[:1] * (y[:, unstriped(yp)] - y[:, unstriped(ym)])
    ln = np.sqrt((gx) ** 2 + (gy) ** 2 + 0.1)
    nx = gx / ln
    ny = gy / ln
    return (ln - 1.0) ** 2 + 0.5 * (np.abs(nx * f64(tx) + ny * f64(ty)))

@@ -1,0 +1,158 @@
+from contextlib import ExitStack
+
+import concourse.mybir as mybir
+from concourse.masks import make_identity
+
+K, T, S, N, U = 512, 1024, 512, 128, 512
+P = 128
+PACK = 4
+FLOPS = 2 * K * N * S
+
+F32 = mybir.dt.float32
+BF16 = mybir.dt.bfloat16
+I32 = mybir.dt.int32
+U32 = mybir.dt.uint32
+U16 = mybir.dt.uint16
+U8 = mybir.dt.uint8
+FP8X4 = mybir.dt.float8_e4m3fn_x4
+ACT = mybir.ActivationFunctionType
+ALU = mybir.AluOpType
+
+PIECES = [(0, 256), (256, 384), (384, 512)]
+CHUNKS = U // P
+TURNED = CHUNKS - 1
+
+
+def tile_picked_ysdfnr_loss_p_kernel(tc, x_words, x_scales, w1, half, tx, ty, offs, xp, xm, yp, ym, out):
+    nc = tc.nc
+    with ExitStack() as ctx:
+        keep = ctx.enter_context(tc.tile_pool(name="keep", bufs=1))
+        ring = ctx.enter_context(tc.tile_pool(name="ring", bufs=4))
+        three = ctx.enter_context(tc.tile_pool(name="three", bufs=3))
+        one = ctx.enter_context(tc.tile_pool(name="one", bufs=1))
+        ypsum = ctx.enter_context(tc.psum_pool(name="ypsum", bufs=4))
+        qpsum = ctx.enter_context(tc.psum_pool(name="qpsum", bufs=2))
+        cpsum = ctx.enter_context(tc.psum_pool(name="cpsum", bufs=2))
+
+        lists = {}
+        for name in ("offs", "xp", "xm", "yp", "ym"):
+            lists[name] = keep.tile([P, U // 16], U16, name="list_" + name)
+        words = keep.tile([P, T], U32, name="words", align_bytes=64)
+        scales = keep.tile([P, T], U8, name="scales", align_bytes=64)
+        w_raw = keep.tile([P, PACK, N], F32, name="w_raw")
+        tang = keep.tile([P, 2, U], F32, name="tang")
+        h = keep.tile([P, CHUNKS], F32, name="h")
+        h2 = keep.tile([P, TURNED], F32, name="h2")
+        ident = keep.tile([P, P], F32, name="ident")
+        warm_in = keep.tile([P, 1], F32, name="warm_in")
+        warm_out = keep.tile([P, 1], F32, name="warm_out")
+
+        nc.gpsimd.memset(scales[:].bitcast(I32), 0)
+        nc.gpsimd.memset(warm_in[:], 1.0)
+        nc.sync.dma_start(lists["offs"][:], offs)
+        for q in range(4):
+            queue = nc.sync if q < 2 else nc.scalar
+            queue.dma_start(scales[32 * q : 32 * q + 4, :].bitcast(I32), x_scales[0, 4 * q : 4 * q + 4, :].bitcast(I32))
+        nc.scalar.dma_start(w_raw[:], w1.rearrange("(p j) n -> p j n", j=PACK))
+        nc.sync.dma_start(words[:].bitcast(I32), x_words[0].rearrange("p c r -> p (c r)").bitcast(I32))
+        nc.scalar.activation(warm_out[:], warm_in[:], ACT.Abs_reciprocal_sqrt)
+        nc.sync.dma_start(lists["xm"][:], xm)
+        nc.sync.dma_start(lists["ym"][:], ym)
+        nc.sync.dma_start(lists["xp"][:], xp)
+        nc.sync.dma_start(lists["yp"][:], yp)
+        with nc.allow_non_contiguous_dma(reason="one spacing a partition"):
+            nc.sync.dma_start(h[:], half[0].rearrange("(b p) -> p b", p=P))
+        nc.sync.dma_start(tang[:, 0, :], tx)
+        nc.sync.dma_start(tang[:, 1, :], ty)
+        last = slice(TURNED * P, U)
+        make_identity(nc, ident[:])
+
+        w_bf = keep.tile([P, N, PACK], BF16, name="w_bf", align_bytes=64)
+        w_codes = keep.tile([P, N], U32, name="w_codes", align_bytes=64)
+        w_scales = keep.tile([P, N], U8, name="w_scales", align_bytes=64)
+        x_codes = keep.tile([P, S], U32, name="x_codes", align_bytes=64)
+        x_bytes = keep.tile([P, S], U8, name="x_bytes", align_bytes=64)
+        y = keep.tile([P, S], F32, name="y", align_bytes=64)
+
+        nc.vector.tensor_copy(x_bytes[:], scales[:].indirect(lists["offs"][:]))
+        nc.scalar.copy(w_bf[:], w_raw[:].rearrange("p j n -> p n j"))
+        nc.vector.quantize_mx(out=w_codes[:].bitcast(FP8X4), scales=w_scales[:], in_=w_bf[:].rearrange("p n j -> p (n j)"))
+        for a, b in PIECES:
+            nc.vector.tensor_copy(x_codes[:, a:b], words[:].indirect(lists["offs"][:, a // 16 : b // 16]))
+            acc = ypsum.tile([P, b - a], F32, name="acc")
+            nc.tensor.matmul_mx(out=acc[:], lhsT=w_codes[:].bitcast(FP8X4), lhsT_scale=w_scales[:],
+                                rhs=x_codes[:, a:b].bitcast(FP8X4), rhs_scale=x_bytes[:, a:b], start=True, stop=True)
+            nc.scalar.copy(y[:, a:b], acc[:])
+        nc.scalar.activation(h2[:], h[:, 0:TURNED], ACT.Square)
+        h_row = ypsum.tile([P, P], F32, name="acc")
+        nc.tensor.transpose(h_row[:], h[:, TURNED:CHUNKS].to_broadcast([P, P]), ident[:])
+
+        def differences(c):
+            entries = slice(c * P // 16, (c + 1) * P // 16)
+            minus = three.tile([P, 2, P], F32, name="pair")
+            d = three.tile([P, 2, P], F32, name="pair")
+            nc.vector.tensor_copy(minus[:, 0, :], y[:].indirect(lists["xm"][:, entries]))
+            nc.vector.tensor_copy(minus[:, 1, :], y[:].indirect(lists["ym"][:, entries]))
+            nc.vector.tensor_tensor(d[:, 0, :], y[:].indirect(lists["xp"][:, entries]), minus[:, 0, :], ALU.subtract)
+            nc.vector.tensor_tensor(d[:, 1, :], y[:].indirect(lists["yp"][:, entries]), minus[:, 1, :], ALU.subtract)
+            return d
+
+        def turned_sum(acc, pair):
+            for i in range(2):
+                nc.tensor.matmul(acc[:], pair[:, i, :], ident[:], start=(i == 0), stop=(i == 1), is_transpose=True)
+
+        held = []
+        for c in range(TURNED):
+            cols = slice(c * P, (c + 1) * P)
+            d = differences(c)
+            sq = one.tile([P, 2, P], F32, name="sq")
+            nc.scalar.activation(sq[:], d[:], ACT.Square)
+            dt = ring.tile([P, 2, P], F32, name="dt")
+            nc.vector.tensor_tensor(dt[:], d[:], tang[:, :, cols], ALU.mult)
+            qT = qpsum.tile([P, P], F32, name="qT")
+            cT = cpsum.tile([P, P], F32, name="cT")
+            turned_sum(qT, sq)
+            turned_sum(cT, dt)
+            r = ring.tile([P, P], F32, name="r")
+            r2 = ring.tile([P, P], F32, name="r2")
+            ln = ring.tile([P, P], F32, name="ln")
+            dot = ring.tile([P, P], F32, name="dot")
+            terms = ring.tile([P, 2, P], F32, name="terms")
+            nc.scalar.activation(r[:], qT[:], ACT.Abs_reciprocal_sqrt, bias=0.1, scale=h2[:, c : c + 1])
+            nc.scalar.activation(r2[:], r[:], ACT.Square)
+            nc.scalar.activation(dot[:], cT[:], ACT.Abs, scale=h[:, c : c + 1])
+            nc.scalar.activation(ln[:], r2[:], ACT.Abs_reciprocal_sqrt)
+            nc.scalar.activation(terms[:, 0, :], ln[:], ACT.Square, bias=-1.0)
+            held.append((cols, terms, dot, r))
+
+        d = differences(TURNED)
+        sq = one.tile([P, 2, P], F32, name="sq")
+        dt = ring.tile([P, 2, P], F32, name="dt")
+        g = keep.tile([P, 2, P], F32, name="g")
+        for i in range(2):
+            nc.vector.tensor_tensor(g[:, i, :], h_row[:], d[:, i, :], ALU.mult)
+            nc.scalar.activation(sq[:, i, :], g[:, i, :], ACT.Square)
+        nc.vector.tensor_tensor(dt[:], g[:], tang[:, :, last], ALU.mult)
+        s = keep.tile([P, P], F32, name="s")
+        cdot = keep.tile([P, P], F32, name="cdot")
+        dot_last = keep.tile([P, P], F32, name="dot_last")
+        r_last = keep.tile([P, P], F32, name="r_last")
+        e = keep.tile([P, P], F32, name="e")
+        f = keep.tile([P, P], F32, name="f")
+        res_last = keep.tile([P, P], F32, name="res_last")
+        nc.vector.tensor_tensor(s[:], sq[:, 0, :], sq[:, 1, :], ALU.add)
+        nc.vector.tensor_tensor(cdot[:], dt[:, 0, :], dt[:, 1, :], ALU.add)
+        nc.scalar.activation(dot_last[:], cdot[:], ACT.Abs, scale=0.5)
+        nc.scalar.activation(r_last[:], s[:], ACT.Abs_reciprocal_sqrt, bias=0.1)
+        nc.vector.scalar_tensor_tensor(e[:], s[:], -2.0, dot_last[:], ALU.mult, ALU.add)
+        nc.vector.scalar_tensor_tensor(f[:], e[:], -0.2, r_last[:], ALU.add, ALU.mult)
+        nc.vector.scalar_tensor_tensor(res_last[:], s[:], 1.1, f[:], ALU.add, ALU.add)
+        nc.sync.dma_start(out[:, last], res_last[:])
+
+        for cols, terms, dot, r in held:
+            nc.vector.scalar_tensor_tensor(terms[:, 1, :], dot[:], 0.5, r[:], ALU.mult, ALU.mult)
+            res_ps = ypsum.tile([P, P], F32, name="acc")
+            turned_sum(res_ps, terms)
+            res = ring.tile([P, P], F32, name="res")
+            nc.scalar.copy(res[:], res_ps[:])
+            nc.sync.dma_start(out[:, cols], res[:])

@@ -28,8 +28,6 @@ def tile_picked_ysdfnr_loss_p_kernel(tc, x_words, x_scales, w1, half, tx, ty, of
     with ExitStack() as ctx:
         keep = ctx.enter_context(tc.tile_pool(name="keep", bufs=1))
         ring = ctx.enter_context(tc.tile_pool(name="ring", bufs=4))
-        three = ctx.enter_context(tc.tile_pool(name="three", bufs=3))
-        one = ctx.enter_context(tc.tile_pool(name="one", bufs=1))
         ypsum = ctx.enter_context(tc.psum_pool(name="ypsum", bufs=4))
         qpsum = ctx.enter_context(tc.psum_pool(name="qpsum", bufs=2))
         cpsum = ctx.enter_context(tc.psum_pool(name="cpsum", bufs=2))
@@ -43,12 +41,18 @@ def tile_picked_ysdfnr_loss_p_kernel(tc, x_words, x_scales, w1, half, tx, ty, of
         tang = keep.tile([P, 2, U], F32, name="tang")
         h = keep.tile([P, CHUNKS], F32, name="h")
         h2 = keep.tile([P, TURNED], F32, name="h2")
+        h2_row = keep.tile([P, P], F32, name="h2_row")
+        h_half = keep.tile([P, P], F32, name="h_half")
+        th = keep.tile([P, 2, P], F32, name="th")
+        h_blocks = keep.tile([P, P], F32, name="h_blocks")
         ident = keep.tile([P, P], F32, name="ident")
         warm_in = keep.tile([P, 1], F32, name="warm_in")
         warm_out = keep.tile([P, 1], F32, name="warm_out")
 
         nc.gpsimd.memset(scales[:].bitcast(I32), 0)
         nc.gpsimd.memset(warm_in[:], 1.0)
+        nc.gpsimd.memset(h_blocks[:], 0.0)
+        nc.gpsimd.dma_start(h_blocks[0:CHUNKS, :], half[0].rearrange("(b p) -> b p", p=P))
         nc.sync.dma_start(lists["offs"][:], offs)
         for q in range(4):
             queue = nc.sync if q < 2 else nc.scalar
@@ -56,14 +60,12 @@ def tile_picked_ysdfnr_loss_p_kernel(tc, x_words, x_scales, w1, half, tx, ty, of
         nc.scalar.dma_start(w_raw[:], w1.rearrange("(p j) n -> p j n", j=PACK))
         nc.sync.dma_start(words[:].bitcast(I32), x_words[0].rearrange("p c r -> p (c r)").bitcast(I32))
         nc.scalar.activation(warm_out[:], warm_in[:], ACT.Abs_reciprocal_sqrt)
-        nc.sync.dma_start(lists["xm"][:], xm)
-        nc.sync.dma_start(lists["ym"][:], ym)
-        nc.sync.dma_start(lists["xp"][:], xp)
-        nc.sync.dma_start(lists["yp"][:], yp)
-        with nc.allow_non_contiguous_dma(reason="one spacing a partition"):
-            nc.sync.dma_start(h[:], half[0].rearrange("(b p) -> p b", p=P))
         nc.sync.dma_start(tang[:, 0, :], tx)
         nc.sync.dma_start(tang[:, 1, :], ty)
+        nc.sync.dma_start(lists["xp"][:], xp)
+        nc.sync.dma_start(lists["xm"][:], xm)
+        nc.sync.dma_start(lists["ym"][:], ym)
+        nc.sync.dma_start(lists["yp"][:], yp)
         last = slice(TURNED * P, U)
         make_identity(nc, ident[:])
 
@@ -74,85 +76,108 @@ def tile_picked_ysdfnr_loss_p_kernel(tc, x_words, x_scales, w1, half, tx, ty, of
         x_bytes = keep.tile([P, S], U8, name="x_bytes", align_bytes=64)
         y = keep.tile([P, S], F32, name="y", align_bytes=64)
 
+        h_turned = qpsum.tile([P, P], F32, name="qT")
+        nc.tensor.transpose(h_turned[:], h_blocks[:], ident[:])
+        nc.scalar.copy(h[:], h_turned[:, 0:CHUNKS])
+        nc.scalar.activation(h2[:], h_turned[:, 0:TURNED], ACT.Square)
+        h_row = cpsum.tile([P, P], F32, name="cT")
+        nc.tensor.transpose(h_row[:], h[:, TURNED:CHUNKS].to_broadcast([P, P]), ident[:])
         nc.vector.tensor_copy(x_bytes[:], scales[:].indirect(lists["offs"][:]))
         nc.scalar.copy(w_bf[:], w_raw[:].rearrange("p j n -> p n j"))
         nc.vector.quantize_mx(out=w_codes[:].bitcast(FP8X4), scales=w_scales[:], in_=w_bf[:].rearrange("p n j -> p (n j)"))
+        nc.scalar.activation(h_half[:], h_row[:], ACT.Copy, scale=0.5)
+        nc.scalar.activation(h2_row[:], h_row[:], ACT.Square)
         for a, b in PIECES:
             nc.vector.tensor_copy(x_codes[:, a:b], words[:].indirect(lists["offs"][:, a // 16 : b // 16]))
             acc = ypsum.tile([P, b - a], F32, name="acc")
             nc.tensor.matmul_mx(out=acc[:], lhsT=w_codes[:].bitcast(FP8X4), lhsT_scale=w_scales[:],
                                 rhs=x_codes[:, a:b].bitcast(FP8X4), rhs_scale=x_bytes[:, a:b], start=True, stop=True)
             nc.scalar.copy(y[:, a:b], acc[:])
-        nc.scalar.activation(h2[:], h[:, 0:TURNED], ACT.Square)
-        h_row = ypsum.tile([P, P], F32, name="acc")
-        nc.tensor.transpose(h_row[:], h[:, TURNED:CHUNKS].to_broadcast([P, P]), ident[:])
+        for i in range(2):
+            nc.gpsimd.tensor_tensor(th[:, i, :], tang[:, i, last], h_half[:], ALU.mult)
+
+        trio = [keep.tile([P, 2, P], F32, name="trio%d" % i) for i in range(3)]
+        duo = [keep.tile([P, 2, P], F32, name="duo%d" % i) for i in range(2)]
+
+        minus = [keep.tile([P, P], F32, name="minus%d" % i) for i in range(2)]
 
         def differences(c):
             entries = slice(c * P // 16, (c + 1) * P // 16)
-            minus = three.tile([P, 2, P], F32, name="pair")
-            d = three.tile([P, 2, P], F32, name="pair")
-            nc.vector.tensor_copy(minus[:, 0, :], y[:].indirect(lists["xm"][:, entries]))
-            nc.vector.tensor_copy(minus[:, 1, :], y[:].indirect(lists["ym"][:, entries]))
-            nc.vector.tensor_tensor(d[:, 0, :], y[:].indirect(lists["xp"][:, entries]), minus[:, 0, :], ALU.subtract)
-            nc.vector.tensor_tensor(d[:, 1, :], y[:].indirect(lists["yp"][:, entries]), minus[:, 1, :], ALU.subtract)
+            d = trio[(2 * c) % 3]
+            axes = (0, 1) if c % 2 == 0 else (1, 0)
+            for place, i in enumerate(axes):
+                nc.vector.tensor_copy(minus[place][:], y[:].indirect(lists[("xm", "ym")[i]][:, entries]))
+            for place, i in enumerate(axes):
+                nc.vector.tensor_tensor(d[:, i, :], y[:].indirect(lists[("xp", "yp")[i]][:, entries]), minus[place][:], ALU.subtract)
             return d
 
         def turned_sum(acc, pair):
             for i in range(2):
                 nc.tensor.matmul(acc[:], pair[:, i, :], ident[:], start=(i == 0), stop=(i == 1), is_transpose=True)
 
-        held = []
-        for c in range(TURNED):
+        def front(c):
             cols = slice(c * P, (c + 1) * P)
             d = differences(c)
-            sq = one.tile([P, 2, P], F32, name="sq")
+            sq = duo[c % 2]
+            dt = duo[(c + 1) % 2]
             nc.scalar.activation(sq[:], d[:], ACT.Square)
-            dt = ring.tile([P, 2, P], F32, name="dt")
             nc.vector.tensor_tensor(dt[:], d[:], tang[:, :, cols], ALU.mult)
             qT = qpsum.tile([P, P], F32, name="qT")
             cT = cpsum.tile([P, P], F32, name="cT")
             turned_sum(qT, sq)
             turned_sum(cT, dt)
-            r = ring.tile([P, P], F32, name="r")
+            rd = trio[(2 * c + 1) % 3]
             r2 = ring.tile([P, P], F32, name="r2")
             ln = ring.tile([P, P], F32, name="ln")
-            dot = ring.tile([P, P], F32, name="dot")
             terms = ring.tile([P, 2, P], F32, name="terms")
-            nc.scalar.activation(r[:], qT[:], ACT.Abs_reciprocal_sqrt, bias=0.1, scale=h2[:, c : c + 1])
-            nc.scalar.activation(r2[:], r[:], ACT.Square)
-            nc.scalar.activation(dot[:], cT[:], ACT.Abs, scale=h[:, c : c + 1])
+            nc.scalar.activation(rd[:, 0, :], qT[:], ACT.Abs_reciprocal_sqrt, bias=0.1, scale=h2[:, c : c + 1])
+            nc.scalar.activation(rd[:, 1, :], cT[:], ACT.Abs, scale=h[:, c : c + 1])
+            nc.scalar.activation(r2[:], rd[:, 0, :], ACT.Square)
             nc.scalar.activation(ln[:], r2[:], ACT.Abs_reciprocal_sqrt)
             nc.scalar.activation(terms[:, 0, :], ln[:], ACT.Square, bias=-1.0)
-            held.append((cols, terms, dot, r))
+            return terms
 
-        d = differences(TURNED)
-        sq = one.tile([P, 2, P], F32, name="sq")
-        dt = ring.tile([P, 2, P], F32, name="dt")
-        g = keep.tile([P, 2, P], F32, name="g")
-        for i in range(2):
-            nc.vector.tensor_tensor(g[:, i, :], h_row[:], d[:, i, :], ALU.mult)
-            nc.scalar.activation(sq[:, i, :], g[:, i, :], ACT.Square)
-        nc.vector.tensor_tensor(dt[:], g[:], tang[:, :, last], ALU.mult)
-        s = keep.tile([P, P], F32, name="s")
-        cdot = keep.tile([P, P], F32, name="cdot")
-        dot_last = keep.tile([P, P], F32, name="dot_last")
-        r_last = keep.tile([P, P], F32, name="r_last")
-        e = keep.tile([P, P], F32, name="e")
-        f = keep.tile([P, P], F32, name="f")
-        res_last = keep.tile([P, P], F32, name="res_last")
-        nc.vector.tensor_tensor(s[:], sq[:, 0, :], sq[:, 1, :], ALU.add)
-        nc.vector.tensor_tensor(cdot[:], dt[:, 0, :], dt[:, 1, :], ALU.add)
-        nc.scalar.activation(dot_last[:], cdot[:], ACT.Abs, scale=0.5)
-        nc.scalar.activation(r_last[:], s[:], ACT.Abs_reciprocal_sqrt, bias=0.1)
-        nc.vector.scalar_tensor_tensor(e[:], s[:], -2.0, dot_last[:], ALU.mult, ALU.add)
-        nc.vector.scalar_tensor_tensor(f[:], e[:], -0.2, r_last[:], ALU.add, ALU.mult)
-        nc.vector.scalar_tensor_tensor(res_last[:], s[:], 1.1, f[:], ALU.add, ALU.add)
-        nc.sync.dma_start(out[:, last], res_last[:])
+        def tangent_term(c, terms):
+            rd = trio[(2 * c + 1) % 3]
+            nc.vector.scalar_tensor_tensor(terms[:, 1, :], rd[:, 1, :], 0.5, rd[:, 0, :], ALU.mult, ALU.mult)
 
-        for cols, terms, dot, r in held:
-            nc.vector.scalar_tensor_tensor(terms[:, 1, :], dot[:], 0.5, r[:], ALU.mult, ALU.mult)
+        def back(c, terms):
             res_ps = ypsum.tile([P, P], F32, name="acc")
             turned_sum(res_ps, terms)
             res = ring.tile([P, P], F32, name="res")
             nc.scalar.copy(res[:], res_ps[:])
-            nc.sync.dma_start(out[:, cols], res[:])
+            nc.sync.dma_start(out[:, c * P : (c + 1) * P], res[:])
+
+        terms0 = front(0)
+        terms1 = front(1)
+        tangent_term(0, terms0)
+        back(0, terms0)
+        terms2 = front(2)
+        tangent_term(1, terms1)
+
+        d = differences(TURNED)
+        sq = duo[TURNED % 2]
+        dt = keep.tile([P, 2, P], F32, name="dt")
+        for i in (1, 0):
+            nc.scalar.activation(sq[:, i, :], d[:, i, :], ACT.Square)
+            nc.vector.tensor_tensor(dt[:, i, :], d[:, i, :], th[:, i, :], ALU.mult)
+        tangent_term(2, terms2)
+        q = keep.tile([P, P], F32, name="q")
+        s = keep.tile([P, P], F32, name="s")
+        cdot = keep.tile([P, P], F32, name="cdot")
+        dot_last = sq[:, 0, :]
+        r_last = keep.tile([P, P], F32, name="r_last")
+        e = keep.tile([P, P], F32, name="e")
+        f = keep.tile([P, P], F32, name="f")
+        res_last = keep.tile([P, P], F32, name="res_last")
+        nc.vector.tensor_tensor(q[:], sq[:, 0, :], sq[:, 1, :], ALU.add)
+        nc.vector.tensor_tensor(cdot[:], dt[:, 0, :], dt[:, 1, :], ALU.add)
+        nc.vector.tensor_tensor(s[:], q[:], h2_row[:], ALU.mult)
+        nc.scalar.activation(dot_last, cdot[:], ACT.Abs)
+        nc.scalar.activation(r_last[:], s[:], ACT.Abs_reciprocal_sqrt, bias=0.1)
+        nc.vector.scalar_tensor_tensor(e[:], s[:], -2.0, dot_last, ALU.mult, ALU.add)
+        nc.vector.scalar_tensor_tensor(f[:], e[:], -0.2, r_last[:], ALU.add, ALU.mult)
+        nc.vector.scalar_tensor_tensor(res_last[:], s[:], 1.1, f[:], ALU.add, ALU.add)
+        nc.sync.dma_start(out[:, last], res_last[:])
+        back(1, terms1)
+        back(2, terms2)

@@ -39,10 +39,10 @@ def tile_picked_ysdfnr_loss_p_kernel(tc, x_words, x_scales, w1, half, tx, ty, of
         scales = keep.tile([P, T], U8, name="scales", align_bytes=64)
         w_raw = keep.tile([P, PACK, N], F32, name="w_raw")
         tang = keep.tile([P, 2, U], F32, name="tang")
-        h = keep.tile([P, CHUNKS], F32, name="h")
+        h = keep.tile([P, TURNED], F32, name="h")
         h2 = keep.tile([P, TURNED], F32, name="h2")
         h2_row = keep.tile([P, P], F32, name="h2_row")
-        h_half = keep.tile([P, P], F32, name="h_half")
+        h_row = keep.tile([P, P], F32, name="h_row")
         th = keep.tile([P, 2, P], F32, name="th")
         h_blocks = keep.tile([P, P], F32, name="h_blocks")
         ident = keep.tile([P, P], F32, name="ident")
@@ -52,21 +52,22 @@ def tile_picked_ysdfnr_loss_p_kernel(tc, x_words, x_scales, w1, half, tx, ty, of
         nc.gpsimd.memset(scales[:].bitcast(I32), 0)
         nc.gpsimd.memset(warm_in[:], 1.0)
         nc.gpsimd.memset(h_blocks[:], 0.0)
-        nc.gpsimd.dma_start(h_blocks[0:CHUNKS, :], half[0].rearrange("(b p) -> b p", p=P))
         nc.sync.dma_start(lists["offs"][:], offs)
         for q in range(4):
             queue = nc.sync if q < 2 else nc.scalar
             queue.dma_start(scales[32 * q : 32 * q + 4, :].bitcast(I32), x_scales[0, 4 * q : 4 * q + 4, :].bitcast(I32))
-        nc.scalar.dma_start(w_raw[:], w1.rearrange("(p j) n -> p j n", j=PACK))
+        nc.sync.dma_start(w_raw[:], w1.rearrange("(p j) n -> p j n", j=PACK))
         nc.sync.dma_start(words[:].bitcast(I32), x_words[0].rearrange("p c r -> p (c r)").bitcast(I32))
         nc.scalar.activation(warm_out[:], warm_in[:], ACT.Abs_reciprocal_sqrt)
         nc.sync.dma_start(tang[:, 0, :], tx)
         nc.sync.dma_start(tang[:, 1, :], ty)
+        last = slice(TURNED * P, U)
+        nc.sync.dma_start(h_blocks[0:CHUNKS, :], half[0].rearrange("(b p) -> b p", p=P))
+        nc.sync.dma_start(h_row[:], half[:, last])
         nc.sync.dma_start(lists["xp"][:], xp)
         nc.sync.dma_start(lists["xm"][:], xm)
         nc.sync.dma_start(lists["ym"][:], ym)
         nc.sync.dma_start(lists["yp"][:], yp)
-        last = slice(TURNED * P, U)
         make_identity(nc, ident[:])
 
         w_bf = keep.tile([P, N, PACK], BF16, name="w_bf", align_bytes=64)
@@ -78,14 +79,11 @@ def tile_picked_ysdfnr_loss_p_kernel(tc, x_words, x_scales, w1, half, tx, ty, of
 
         h_turned = qpsum.tile([P, P], F32, name="qT")
         nc.tensor.transpose(h_turned[:], h_blocks[:], ident[:])
-        nc.scalar.copy(h[:], h_turned[:, 0:CHUNKS])
+        nc.scalar.copy(h[:], h_turned[:, 0:TURNED])
         nc.scalar.activation(h2[:], h_turned[:, 0:TURNED], ACT.Square)
-        h_row = cpsum.tile([P, P], F32, name="cT")
-        nc.tensor.transpose(h_row[:], h[:, TURNED:CHUNKS].to_broadcast([P, P]), ident[:])
         nc.vector.tensor_copy(x_bytes[:], scales[:].indirect(lists["offs"][:]))
         nc.scalar.copy(w_bf[:], w_raw[:].rearrange("p j n -> p n j"))
         nc.vector.quantize_mx(out=w_codes[:].bitcast(FP8X4), scales=w_scales[:], in_=w_bf[:].rearrange("p n j -> p (n j)"))
-        nc.scalar.activation(h_half[:], h_row[:], ACT.Copy, scale=0.5)
         nc.scalar.activation(h2_row[:], h_row[:], ACT.Square)
         for a, b in PIECES:
             nc.vector.tensor_copy(x_codes[:, a:b], words[:].indirect(lists["offs"][:, a // 16 : b // 16]))
@@ -94,7 +92,7 @@ def tile_picked_ysdfnr_loss_p_kernel(tc, x_words, x_scales, w1, half, tx, ty, of
                                 rhs=x_codes[:, a:b].bitcast(FP8X4), rhs_scale=x_bytes[:, a:b], start=True, stop=True)
             nc.scalar.copy(y[:, a:b], acc[:])
         for i in range(2):
-            nc.gpsimd.tensor_tensor(th[:, i, :], tang[:, i, last], h_half[:], ALU.mult)
+            nc.gpsimd.tensor_tensor(th[:, i, :], tang[:, i, last], h_row[:], ALU.mult)
 
         trio = [keep.tile([P, 2, P], F32, name="trio%d" % i) for i in range(3)]
         duo = [keep.tile([P, 2, P], F32, name="duo%d" % i) for i in range(2)]
@@ -173,7 +171,7 @@ def tile_picked_ysdfnr_loss_p_kernel(tc, x_words, x_scales, w1, half, tx, ty, of
         nc.vector.tensor_tensor(q[:], sq[:, 0, :], sq[:, 1, :], ALU.add)
         nc.vector.tensor_tensor(cdot[:], dt[:, 0, :], dt[:, 1, :], ALU.add)
         nc.vector.tensor_tensor(s[:], q[:], h2_row[:], ALU.mult)
-        nc.scalar.activation(dot_last, cdot[:], ACT.Abs)
+        nc.scalar.activation(dot_last, cdot[:], ACT.Abs, scale=0.5)
         nc.scalar.activation(r_last[:], s[:], ACT.Abs_reciprocal_sqrt, bias=0.1)
         nc.vector.scalar_tensor_tensor(e[:], s[:], -2.0, dot_last, ALU.mult, ALU.add)
         nc.vector.scalar_tensor_tensor(f[:], e[:], -0.2, r_last[:], ALU.add, ALU.mult)

from contextlib import ExitStack

import concourse.mybir as mybir
from concourse.masks import make_identity

K, T, S, N, U = 512, 1024, 512, 128, 512
P = 128
PACK = 4
FLOPS = 2 * K * N * S

F32 = mybir.dt.float32
BF16 = mybir.dt.bfloat16
I32 = mybir.dt.int32
U32 = mybir.dt.uint32
U16 = mybir.dt.uint16
U8 = mybir.dt.uint8
FP8X4 = mybir.dt.float8_e4m3fn_x4
ACT = mybir.ActivationFunctionType
ALU = mybir.AluOpType

PIECES = [(0, 256), (256, 384), (384, 512)]
CHUNKS = U // P
TURNED = CHUNKS - 1


def tile_picked_ysdfnr_loss_p_kernel(tc, x_words, x_scales, w1, half, tx, ty, offs, xp, xm, yp, ym, out):
    nc = tc.nc
    with ExitStack() as ctx:
        keep = ctx.enter_context(tc.tile_pool(name="keep", bufs=1))
        ring = ctx.enter_context(tc.tile_pool(name="ring", bufs=4))
        ypsum = ctx.enter_context(tc.psum_pool(name="ypsum", bufs=4))
        qpsum = ctx.enter_context(tc.psum_pool(name="qpsum", bufs=2))
        cpsum = ctx.enter_context(tc.psum_pool(name="cpsum", bufs=2))

        lists = {}
        for name in ("offs", "xp", "xm", "yp", "ym"):
            lists[name] = keep.tile([P, U // 16], U16, name="list_" + name)
        words = keep.tile([P, T], U32, name="words", align_bytes=64)
        scales = keep.tile([P, T], U8, name="scales", align_bytes=64)
        w_raw = keep.tile([P, PACK, N], F32, name="w_raw")
        tang = keep.tile([P, 2, U], F32, name="tang")
        h = keep.tile([P, TURNED], F32, name="h")
        h2 = keep.tile([P, TURNED], F32, name="h2")
        h2_row = keep.tile([P, P], F32, name="h2_row")
        h_row = keep.tile([P, P], F32, name="h_row")
        th = keep.tile([P, 2, P], F32, name="th")
        h_blocks = keep.tile([P, P], F32, name="h_blocks")
        ident = keep.tile([P, P], F32, name="ident")
        warm_in = keep.tile([P, 1], F32, name="warm_in")
        warm_out = keep.tile([P, 1], F32, name="warm_out")

        nc.gpsimd.memset(scales[:].bitcast(I32), 0)
        nc.gpsimd.memset(warm_in[:], 1.0)
        nc.gpsimd.memset(h_blocks[:], 0.0)
        nc.sync.dma_start(lists["offs"][:], offs)
        for q in range(4):
            queue = nc.sync if q < 2 else nc.scalar
            queue.dma_start(scales[32 * q : 32 * q + 4, :].bitcast(I32), x_scales[0, 4 * q : 4 * q + 4, :].bitcast(I32))
        nc.sync.dma_start(w_raw[:], w1.rearrange("(p j) n -> p j n", j=PACK))
        nc.sync.dma_start(words[:].bitcast(I32), x_words[0].rearrange("p c r -> p (c r)").bitcast(I32))
        nc.scalar.activation(warm_out[:], warm_in[:], ACT.Abs_reciprocal_sqrt)
        nc.sync.dma_start(tang[:, 0, :], tx)
        nc.sync.dma_start(tang[:, 1, :], ty)
        last = slice(TURNED * P, U)
        nc.sync.dma_start(h_blocks[0:CHUNKS, :], half[0].rearrange("(b p) -> b p", p=P))
        nc.sync.dma_start(h_row[:], half[:, last])
        nc.sync.dma_start(lists["xp"][:], xp)
        nc.sync.dma_start(lists["xm"][:], xm)
        nc.sync.dma_start(lists["ym"][:], ym)
        nc.sync.dma_start(lists["yp"][:], yp)
        make_identity(nc, ident[:])

        w_bf = keep.tile([P, N, PACK], BF16, name="w_bf", align_bytes=64)
        w_codes = keep.tile([P, N], U32, name="w_codes", align_bytes=64)
        w_scales = keep.tile([P, N], U8, name="w_scales", align_bytes=64)
        x_codes = keep.tile([P, S], U32, name="x_codes", align_bytes=64)
        x_bytes = keep.tile([P, S], U8, name="x_bytes", align_bytes=64)
        y = keep.tile([P, S], F32, name="y", align_bytes=64)

        h_turned = qpsum.tile([P, P], F32, name="qT")
        nc.tensor.transpose(h_turned[:], h_blocks[:], ident[:])
        nc.scalar.copy(h[:], h_turned[:, 0:TURNED])
        nc.scalar.activation(h2[:], h_turned[:, 0:TURNED], ACT.Square)
        nc.vector.tensor_copy(x_bytes[:], scales[:].indirect(lists["offs"][:]))
        nc.scalar.copy(w_bf[:], w_raw[:].rearrange("p j n -> p n j"))
        nc.vector.quantize_mx(out=w_codes[:].bitcast(FP8X4), scales=w_scales[:], in_=w_bf[:].rearrange("p n j -> p (n j)"))
        nc.scalar.activation(h2_row[:], h_row[:], ACT.Square)
        for a, b in PIECES:
            nc.vector.tensor_copy(x_codes[:, a:b], words[:].indirect(lists["offs"][:, a // 16 : b // 16]))
            acc = ypsum.tile([P, b - a], F32, name="acc")
            nc.tensor.matmul_mx(out=acc[:], lhsT=w_codes[:].bitcast(FP8X4), lhsT_scale=w_scales[:],
                                rhs=x_codes[:, a:b].bitcast(FP8X4), rhs_scale=x_bytes[:, a:b], start=True, stop=True)
            nc.scalar.copy(y[:, a:b], acc[:])
        for i in range(2):
            nc.gpsimd.tensor_tensor(th[:, i, :], tang[:, i, last], h_row[:], ALU.mult)

        trio = [keep.tile([P, 2, P], F32, name="trio%d" % i) for i in range(3)]
        duo = [keep.tile([P, 2, P], F32, name="duo%d" % i) for i in range(2)]

        minus = [keep.tile([P, P], F32, name="minus%d" % i) for i in range(2)]

        def differences(c):
            entries = slice(c * P // 16, (c + 1) * P // 16)
            d = trio[(2 * c) % 3]
            axes = (0, 1) if c % 2 == 0 else (1, 0)
            for place, i in enumerate(axes):
                nc.vector.tensor_copy(minus[place][:], y[:].indirect(lists[("xm", "ym")[i]][:, entries]))
            for place, i in enumerate(axes):
                nc.vector.tensor_tensor(d[:, i, :], y[:].indirect(lists[("xp", "yp")[i]][:, entries]), minus[place][:], ALU.subtract)
            return d

        def turned_sum(acc, pair):
            for i in range(2):
                nc.tensor.matmul(acc[:], pair[:, i, :], ident[:], start=(i == 0), stop=(i == 1), is_transpose=True)

        def front(c):
            cols = slice(c * P, (c + 1) * P)
            d = differences(c)
            sq = duo[c % 2]
            dt = duo[(c + 1) % 2]
            nc.scalar.activation(sq[:], d[:], ACT.Square)
            nc.vector.tensor_tensor(dt[:], d[:], tang[:, :, cols], ALU.mult)
            qT = qpsum.tile([P, P], F32, name="qT")
            cT = cpsum.tile([P, P], F32, name="cT")
            turned_sum(qT, sq)
            turned_sum(cT, dt)
            rd = trio[(2 * c + 1) % 3]
            r2 = ring.tile([P, P], F32, name="r2")
            ln = ring.tile([P, P], F32, name="ln")
            terms = ring.tile([P, 2, P], F32, name="terms")
            nc.scalar.activation(rd[:, 0, :], qT[:], ACT.Abs_reciprocal_sqrt, bias=0.1, scale=h2[:, c : c + 1])
            nc.scalar.activation(rd[:, 1, :], cT[:], ACT.Abs, scale=h[:, c : c + 1])
            nc.scalar.activation(r2[:], rd[:, 0, :], ACT.Square)
            nc.scalar.activation(ln[:], r2[:], ACT.Abs_reciprocal_sqrt)
            nc.scalar.activation(terms[:, 0, :], ln[:], ACT.Square, bias=-1.0)
            return terms

        def tangent_term(c, terms):
            rd = trio[(2 * c + 1) % 3]
            nc.vector.scalar_tensor_tensor(terms[:, 1, :], rd[:, 1, :], 0.5, rd[:, 0, :], ALU.mult, ALU.mult)

        def back(c, terms):
            res_ps = ypsum.tile([P, P], F32, name="acc")
            turned_sum(res_ps, terms)
            res = ring.tile([P, P], F32, name="res")
            nc.scalar.copy(res[:], res_ps[:])
            nc.sync.dma_start(out[:, c * P : (c + 1) * P], res[:])

        terms0 = front(0)
        terms1 = front(1)
        tangent_term(0, terms0)
        back(0, terms0)
        terms2 = front(2)
        tangent_term(1, terms1)

        d = differences(TURNED)
        sq = duo[TURNED % 2]
        dt = keep.tile([P, 2, P], F32, name="dt")
        for i in (1, 0):
            nc.scalar.activation(sq[:, i, :], d[:, i, :], ACT.Square)
            nc.vector.tensor_tensor(dt[:, i, :], d[:, i, :], th[:, i, :], ALU.mult)
        tangent_term(2, terms2)
        q = keep.tile([P, P], F32, name="q")
        s = keep.tile([P, P], F32, name="s")
        cdot = keep.tile([P, P], F32, name="cdot")
        dot_last = sq[:, 0, :]
        r_last = keep.tile([P, P], F32, name="r_last")
        e = keep.tile([P, P], F32, name="e")
        f = keep.tile([P, P], F32, name="f")
        res_last = keep.tile([P, P], F32, name="res_last")
        nc.vector.tensor_tensor(q[:], sq[:, 0, :], sq[:, 1, :], ALU.add)
        nc.vector.tensor_tensor(cdot[:], dt[:, 0, :], dt[:, 1, :], ALU.add)
        nc.vector.tensor_tensor(s[:], q[:], h2_row[:], ALU.mult)
        nc.scalar.activation(dot_last, cdot[:], ACT.Abs, scale=0.5)
        nc.scalar.activation(r_last[:], s[:], ACT.Abs_reciprocal_sqrt, bias=0.1)
        nc.vector.scalar_tensor_tensor(e[:], s[:], -2.0, dot_last, ALU.mult, ALU.add)
        nc.vector.scalar_tensor_tensor(f[:], e[:], -0.2, r_last[:], ALU.add, ALU.mult)
        nc.vector.scalar_tensor_tensor(res_last[:], s[:], 1.1, f[:], ALU.add, ALU.add)
        nc.sync.dma_start(out[:, last], res_last[:])
        back(1, terms1)
        back(2, terms2)
